import numpy as np
import ml_dtypes


def mxq(x, axis, fmt="e4m3"):
    dtype, down = {"e4m3": (ml_dtypes.float8_e4m3fn, 7), "e5m2": (ml_dtypes.float8_e5m2, 14)}[fmt]
    v = np.moveaxis(np.asarray(x, np.float32).astype(ml_dtypes.bfloat16).astype(np.float64), axis, -1)
    blocks = v.reshape(v.shape[:-1] + (-1, 32))
    amax = np.abs(blocks).max(-1, keepdims=True)
    byte = np.maximum(np.where(amax > 0, np.frexp(amax)[1] - 1 + 127, 0) - down, 1)
    scale = np.exp2(byte - 127.0)
    codes = (blocks / scale).astype(np.float32).astype(dtype).astype(np.float64)
    return np.moveaxis((codes * scale).reshape(v.shape), -1, axis)


WIDE = False


def mx_kscale(k):
    if not WIDE:
        return np.ones(k)
    levels = np.array([10, -10, 5, -5, 0])
    if k % 512:
        return np.exp2(np.random.permutation(np.resize(levels, k // 32))).repeat(32)
    a = np.empty((k // 512, 16))
    for p in range(k // 512):
        a[p, :8] = np.random.permutation(np.resize(levels, 8))
        for g in range(8):
            far = levels[np.abs(levels - a[p, g]) >= 10]
            a[p, g + 8] = far[np.random.randint(len(far))]
    return np.exp2(a.ravel()).repeat(32)


def f64(x):
    return np.asarray(x).astype(np.float64)


def striped(idx):
    return np.tile(np.asarray(idx).reshape(-1, 16).T, (8, 1)).astype(np.uint16)


def unstriped(offs):
    return offs[:16].T.reshape(-1).astype(np.int64)


E2M1 = np.array([0.0, 0.5, 1.0, 1.5, 2.0, 3.0, 4.0, 6.0, -0.0, -0.5, -1.0, -1.5, -2.0, -3.0, -4.0, -6.0])


def pack_weight(w, fmt):
    k, n = w.shape
    w = f64(np.asarray(w, np.float32).astype(ml_dtypes.bfloat16)).reshape(k // 32, 32, n)
    amax = np.abs(w).max(1)
    if fmt == "e4m3":
        byte = np.frexp(amax)[1] - 1 + 127 - 7
    else:
        mant, ex = np.frexp(amax / 6.0)
        byte = np.where(mant > 0.5, ex, ex - 1) + 127
    byte = np.clip(np.where(amax > 0, byte, 1), 1, 254)
    scaled = (w * np.exp2(127.0 - byte)[:, None, :]).reshape(k, n).astype(np.float32)
    by_word = np.ascontiguousarray(scaled.reshape(k // 512, 128, 4, n).transpose(0, 1, 3, 2))
    if fmt == "e4m3":
        words = by_word.astype(ml_dtypes.float8_e4m3fn).view(np.uint8)
    else:
        c = by_word.astype(ml_dtypes.float4_e2m1fn).view(np.uint8) & 0xF
        words = (c[..., 0::2] | (c[..., 1::2] << 4)).reshape(k // 512, 128, 2 * n)
    return np.ascontiguousarray(words), np.ascontiguousarray(byte.astype(np.uint8).reshape(k // 512, 16, n))


def unpack_weight(words, scales, fmt):
    g, _, n = scales.shape
    words = np.ascontiguousarray(words).reshape(g, 128, n, -1)
    if fmt == "e4m3":
        vals = words.view(ml_dtypes.float8_e4m3fn).astype(np.float64)
    else:
        nib = np.empty((g, 128, n, 4), np.uint8)
        nib[..., 0::2] = words & 0xF
        nib[..., 1::2] = words >> 4
        vals = E2M1[nib]
    vals = vals * np.repeat(np.exp2(scales.astype(np.float64) - 127.0), 8, axis=1)[..., None]
    return vals.transpose(0, 1, 3, 2).reshape(g * 512, n)


D, E, T, I, Q, G = 512, 512, 2048, 512, 128, 32


def setup_inputs():
    n = np.random.standard_normal
    idx = np.random.permutation(T)[:I]
    fd = mx_kscale(D)
    fe = mx_kscale(E)
    keysp = pack_weight(n((D, T)) / fd[:, None], "e2m1")
    valsp = pack_weight(n((E, T)) / fe[:, None], "e2m1")
    return {
        "query": (n((D, Q)) * 0.7 / np.sqrt(D) * fd[:, None]).astype(np.float32),
        "keys_words": keysp[0],
        "keys_scales": keysp[1],
        "temper": (np.random.uniform(0.3, 3.0, (Q, 1))).astype(np.float32),
        "gout": (n((E, Q)) * 1 / np.sqrt(E) * fe[:, None]).astype(np.float32),
        "vals_words": valsp[0],
        "vals_scales": valsp[1],
        "size": (np.random.uniform(0.5, 2.0, (1, I))).astype(np.float32),
        "old": (0.5 * n((Q, T))).astype(np.float32),
        "offs": striped(idx),
    }


def reference(query, keys_words, keys_scales, temper, gout, vals_words, vals_scales, size, old, offs):
    idx = unstriped(offs)
    keysu = unpack_weight(keys_words, keys_scales, "e2m1")
    valsu = unpack_weight(vals_words, vals_scales, "e2m1")
    queryq = mxq(f64(query), 0, "e4m3")
    keysidxg = keysu[:, idx]
    a = queryq.T @ keysidxg
    x1 = np.exp(a)
    s = x1.reshape(Q, G, I // G).sum(axis=2)
    p = np.exp(np.log(s) * f64(temper))
    z = np.sum(p, axis=1, keepdims=True)
    sh = p / s / z
    sr = np.repeat(sh, I // G, axis=1)
    goutq = mxq(f64(gout), 0, "e4m3")
    valsidxg = valsu[:, idx]
    c0 = goutq.T @ valsidxg
    dsr = c0 * f64(size) * x1
    dsh = dsr.reshape(Q, G, I // G).sum(axis=2)
    dz = np.sum(dsh * p / s / np.square(z) * (-1.0), axis=1, keepdims=True)
    dp = dsh / z / s + dz
    ds = dp * p * f64(temper) / s - dsh / z * p / np.square(s)
    r1 = np.repeat(ds, I // G, axis=1)
    dx1 = c0 * f64(size) * sr + r1
    da = dx1 * x1
    gs = da * 512.0
    gf = np.zeros((Q, T))
    gf[:, idx] = gs
    y = f64(old) + gf
    return y

@@ -1,0 +1,186 @@
+from contextlib import ExitStack
+
+import concourse.mybir as mybir
+from concourse.masks import make_identity
+
+D, T, I, Q, G = 512, 2048, 512, 128, 32
+PAGE = I // G
+P = 128
+PACK = 4
+FLOPS = 2 * 2 * D * I * Q
+
+F32 = mybir.dt.float32
+BF16 = mybir.dt.bfloat16
+I32 = mybir.dt.int32
+U32 = mybir.dt.uint32
+U16 = mybir.dt.uint16
+U8 = mybir.dt.uint8
+FP8X4 = mybir.dt.float8_e4m3fn_x4
+FP4X4 = mybir.dt.float4_e2m1fn_x4
+ALU = mybir.AluOpType
+ACT = mybir.ActivationFunctionType
+AX = mybir.AxisListType
+
+TINY = 2.0 ** -64
+STORE_WIDTHS = (384, 512, 512, 384, 256)
+
+
+def by_page(ap):
+    return ap.rearrange("p (g j) -> p g j", j=PAGE)
+
+
+def spread(ap):
+    return ap.unsqueeze(2).to_broadcast([P, G, PAGE])
+
+
+def tile_attend_btemperedpages_s_kernel(tc, query, keys_words, keys_scales, temper, gout,
+                                         vals_words, vals_scales, size, old, offs, out):
+    nc = tc.nc
+    with ExitStack() as ctx:
+        sb = ctx.enter_context(tc.tile_pool(name="sb", bufs=1))
+        ps = ctx.enter_context(tc.psum_pool(name="ps", bufs=1))
+
+        offsets = sb.tile([P, I // 16], U16, name="offsets")
+        k_words = sb.tile([P, T], U16, name="k_words", align_bytes=64)
+        v_words = sb.tile([P, T], U16, name="v_words", align_bytes=64)
+        k_bytes = sb.tile([P, T], U8, name="k_bytes", align_bytes=64)
+        v_bytes = sb.tile([P, T], U8, name="v_bytes", align_bytes=64)
+        q_raw = sb.tile([P, PACK, Q], F32, name="q_raw")
+        g_raw = sb.tile([P, PACK, Q], F32, name="g_raw")
+        size_col = sb.tile([P, PACK], F32, name="size_col")
+        tau = sb.tile([P, 1], F32, name="tau")
+        placed = sb.tile([P, T], F32, name="placed")
+        ident = sb.tile([P, P], F32, name="ident")
+        warm = sb.tile([P, 1], F32, name="warm")
+        warm_out = sb.tile([P, 1], F32, name="warm_out")
+
+        nc.gpsimd.memset(k_bytes[:].bitcast(I32), 0)
+        nc.vector.memset(v_bytes[:].bitcast(I32), 0)
+        nc.vector.memset(warm[:], 0.0)
+        nc.scalar.activation(warm_out[:], warm[:], ACT.Exp)
+        make_identity(nc, ident[:])
+        nc.vector.memset(placed[:], 0.0)
+
+        def load_scale_rows(tile, rows):
+            for quad in range(4):
+                nc.sync.dma_start(out=tile[32 * quad:32 * quad + 4, :].bitcast(I32),
+                                  in_=rows[0, 4 * quad:4 * quad + 4, :].bitcast(I32))
+
+        nc.sync.dma_start(offsets[:], offs)
+        nc.sync.dma_start(out=k_words[:].bitcast(I32), in_=keys_words[0].bitcast(I32))
+        load_scale_rows(k_bytes, keys_scales)
+        nc.sync.dma_start(out=q_raw[:], in_=query.rearrange("(p j) q -> p j q", j=PACK))
+        nc.sync.dma_start(out=v_words[:].bitcast(I32), in_=vals_words[0].bitcast(I32))
+        nc.sync.dma_start(out=g_raw[:], in_=gout.rearrange("(p j) q -> p j q", j=PACK))
+        nc.gpsimd.dma_start(out=size_col[:], in_=size.rearrange("o (p j) -> (o p) j", j=PACK))
+        nc.gpsimd.dma_start(out=tau[:], in_=temper)
+        load_scale_rows(v_bytes, vals_scales)
+        old_sb = sb.tile([P, T], F32, name="old_sb")
+        nc.sync.dma_start(out=old_sb[:], in_=old)
+
+        def to_bf16(raw, name):
+            woven = sb.tile([P, Q, PACK], BF16, name=name, align_bytes=64)
+            nc.scalar.copy(out=woven[:].rearrange("p (c i) t -> p c t i", i=4),
+                           in_=raw[:].rearrange("p t (c i) -> p c t i", i=4))
+            return woven
+
+        def quantise(woven, name):
+            codes = sb.tile([P, Q], U32, name=name + "_codes", align_bytes=64)
+            scales = sb.tile([P, Q], U8, name=name + "_scales", align_bytes=64)
+            nc.vector.quantize_mx(out=codes[:].bitcast(FP8X4), scales=scales[:],
+                                  in_=woven[:].rearrange("p q t -> p (q t)"))
+            return codes, scales
+
+        def gather(window, dtype, name):
+            picked = sb.tile([P, I], dtype, name=name, align_bytes=64)
+            nc.vector.tensor_copy(picked[:], window[:].indirect(offsets[:]))
+            return picked
+
+        def product(rows, words, scale_bytes, name):
+            acc = ps.tile([P, I], F32, name=name)
+            nc.tensor.matmul_mx(out=acc[:], lhsT=rows[0][:].bitcast(FP8X4), lhsT_scale=rows[1][:],
+                                rhs=words[:].bitcast(FP4X4), rhs_scale=scale_bytes[:],
+                                start=True, stop=True)
+            return acc
+
+        def small(name, width=G):
+            return sb.tile([P, width], F32, name=name)
+
+        def wide(name):
+            return sb.tile([P, I], F32, name=name)
+
+        q_woven = to_bf16(q_raw, "q_woven")
+        g_woven = to_bf16(g_raw, "g_woven")
+
+        tau_less_one = small("tau_less_one", 1)
+        tau_neg = small("tau_neg", 1)
+        nc.gpsimd.tensor_scalar(tau_less_one[:], tau[:], 1.0, -1.0, ALU.mult, ALU.add)
+        nc.gpsimd.tensor_scalar(tau_neg[:], tau[:], -1.0, 0.0, ALU.mult, ALU.add)
+
+        kw = gather(k_words, U16, "kw")
+        q_mx = quantise(q_woven, "q")
+        kb = gather(k_bytes, U8, "kb")
+        a = product(q_mx, kw, kb, "a")
+        g_mx = quantise(g_woven, "g")
+        a_max_neg = small("a_max_neg", 1)
+        nc.vector.tensor_reduce(a_max_neg[:], a[:], AX.X, ALU.max, negate=True)
+        x = wide("x")
+        nc.scalar.activation(x[:], a[:], ACT.Exp, bias=a_max_neg[:])
+        size_ps = ps.tile([P, PACK, P], F32, name="size_ps")
+        for j in range(PACK):
+            nc.tensor.transpose(size_ps[:, j, :], size_col[:, j:j + 1].to_broadcast([P, P]), ident[:])
+        size_row = wide("size_row")
+        nc.scalar.copy(out=size_row[:].rearrange("p (n j) -> p n j", j=PACK),
+                       in_=size_ps[:].rearrange("p j n -> p n j"))
+
+        vw = gather(v_words, U16, "vw")
+        s = small("s")
+        nc.vector.tensor_reduce(s[:], by_page(x[:]), AX.X, ALU.add)
+        log_s = small("log_s")
+        nc.scalar.activation(log_s[:], s[:], ACT.Ln, bias=TINY)
+        p = small("p")
+        z = small("z", 1)
+        nc.scalar.activation(p[:], log_s[:], ACT.Exp, scale=tau[:], accum_out=z[:])
+        p_over_s = small("p_over_s")
+        nc.scalar.activation(p_over_s[:], log_s[:], ACT.Exp, scale=tau_less_one[:])
+
+        vb = gather(v_bytes, U8, "vb")
+        c0 = product(g_mx, vw, vb, "c0")
+        s_safe = small("s_safe")
+        nc.vector.tensor_scalar(s_safe[:], s[:], TINY, None, ALU.add)
+        s_inv = small("s_inv")
+        nc.vector.reciprocal(s_inv[:], s_safe[:])
+        c = wide("c")
+        nc.vector.tensor_tensor(c[:], c0[:], size_row[:], ALU.mult)
+        cx = wide("cx")
+        nc.vector.tensor_tensor(cx[:], c[:], x[:], ALU.mult)
+        page_cx = small("page_cx")
+        nc.vector.tensor_reduce(page_cx[:], by_page(cx[:]), AX.X, ALU.add)
+        mean_c = small("mean_c")
+        nc.vector.tensor_tensor(mean_c[:], page_cx[:], s_inv[:], ALU.mult)
+        u0 = wide("u0")
+        nc.vector.scalar_tensor_tensor(by_page(u0[:]), spread(mean_c[:]), tau_less_one[:], by_page(c[:]),
+                                       ALU.mult, ALU.add)
+
+        z_inv = small("z_inv", 1)
+        nc.vector.reciprocal(z_inv[:], z[:])
+        weighted = small("weighted")
+        total = small("total", 1)
+        nc.vector.scalar_tensor_tensor(weighted[:], mean_c[:], tau_neg[:], p[:], ALU.mult, ALU.mult,
+                                       accum_out=total[:])
+        shift = small("shift", 1)
+        nc.vector.tensor_scalar(shift[:], total[:], z_inv[:], z_inv[:], ALU.mult, ALU.mult)
+        u = wide("u")
+        nc.scalar.activation(u[:], u0[:], ACT.Identity, bias=shift[:], scale=z_inv[:])
+        w = wide("w")
+        nc.vector.scalar_tensor_tensor(by_page(w[:]), by_page(x[:]), 512.0, spread(p_over_s[:]),
+                                       ALU.mult, ALU.mult)
+        nc.vector.tensor_tensor(placed[:].indirect(offsets[:]), u[:], w[:], ALU.mult)
+
+        col = 0
+        for n, width in enumerate(STORE_WIDTHS):
+            result = sb.tile([P, width], F32, name=f"result{n}")
+            nc.vector.tensor_tensor(result[:], old_sb[:, col:col + width], placed[:, col:col + width], ALU.add)
+            queue = nc.sync if n % 2 == 0 else nc.scalar
+            queue.dma_start(out=out[:, col:col + width], in_=result[:])
+            col = col + width

@@ -22,7 +22,12 @@ ACT = mybir.ActivationFunctionType
 AX = mybir.AxisListType
 
 TINY = 2.0 ** -64
-STORE_WIDTHS = (384, 512, 512, 384, 256)
+HALF = I // 2
+STORE_WIDTHS = (384, 640, 448, 320, 256)
+
+
+def halves():
+    return [(slice(h * HALF, (h + 1) * HALF), slice(h * G // 2, (h + 1) * G // 2)) for h in range(2)]
 
 
 def by_page(ap):
@@ -30,7 +35,7 @@ def by_page(ap):
 
 
 def spread(ap):
-    return ap.unsqueeze(2).to_broadcast([P, G, PAGE])
+    return ap.unsqueeze(2).to_broadcast([P, ap.shape[1], PAGE])
 
 
 def tile_attend_btemperedpages_s_kernel(tc, query, keys_words, keys_scales, temper, gout,
@@ -41,42 +46,33 @@ def tile_attend_btemperedpages_s_kernel(tc, query, keys_words, keys_scales, temp
         ps = ctx.enter_context(tc.psum_pool(name="ps", bufs=1))
 
         offsets = sb.tile([P, I // 16], U16, name="offsets")
-        k_words = sb.tile([P, T], U16, name="k_words", align_bytes=64)
-        v_words = sb.tile([P, T], U16, name="v_words", align_bytes=64)
+        k_words = sb.tile([P, T], U16, name="k_words", tag="k_pool", align_bytes=64)
         k_bytes = sb.tile([P, T], U8, name="k_bytes", align_bytes=64)
         v_bytes = sb.tile([P, T], U8, name="v_bytes", align_bytes=64)
-        q_raw = sb.tile([P, PACK, Q], F32, name="q_raw")
-        g_raw = sb.tile([P, PACK, Q], F32, name="g_raw")
-        size_col = sb.tile([P, PACK], F32, name="size_col")
+        q_raw = sb.tile([P, PACK, Q], F32, name="q_raw", tag="q_stage")
+        g_raw = sb.tile([P, PACK, Q], F32, name="g_raw", tag="g_stage")
+        size_col = sb.tile([P, PACK], F32, name="size_col", tag="v_pool", align_bytes=64)
         tau = sb.tile([P, 1], F32, name="tau")
         placed = sb.tile([P, T], F32, name="placed")
         ident = sb.tile([P, P], F32, name="ident")
-        warm = sb.tile([P, 1], F32, name="warm")
-        warm_out = sb.tile([P, 1], F32, name="warm_out")
 
-        nc.gpsimd.memset(k_bytes[:].bitcast(I32), 0)
-        nc.vector.memset(v_bytes[:].bitcast(I32), 0)
-        nc.vector.memset(warm[:], 0.0)
-        nc.scalar.activation(warm_out[:], warm[:], ACT.Exp)
         make_identity(nc, ident[:])
-        nc.vector.memset(placed[:], 0.0)
+        nc.vector.memset(k_bytes[:].bitcast(I32), 0)
+        nc.vector.memset(placed[:, :T // 2 - 1], 0.0)
+        nc.vector.memset(placed[:, T // 2 - 1:], 0.0)
+        nc.vector.memset(v_bytes[:].bitcast(I32), 0)
 
-        def load_scale_rows(tile, rows):
+        def load_scale_rows(queue, tile, rows):
             for quad in range(4):
-                nc.sync.dma_start(out=tile[32 * quad:32 * quad + 4, :].bitcast(I32),
+                queue.dma_start(out=tile[32 * quad:32 * quad + 4, :].bitcast(I32),
                                   in_=rows[0, 4 * quad:4 * quad + 4, :].bitcast(I32))
 
         nc.sync.dma_start(offsets[:], offs)
         nc.sync.dma_start(out=k_words[:].bitcast(I32), in_=keys_words[0].bitcast(I32))
-        load_scale_rows(k_bytes, keys_scales)
+        load_scale_rows(nc.scalar, k_bytes, keys_scales)
         nc.sync.dma_start(out=q_raw[:], in_=query.rearrange("(p j) q -> p j q", j=PACK))
-        nc.sync.dma_start(out=v_words[:].bitcast(I32), in_=vals_words[0].bitcast(I32))
-        nc.sync.dma_start(out=g_raw[:], in_=gout.rearrange("(p j) q -> p j q", j=PACK))
-        nc.gpsimd.dma_start(out=size_col[:], in_=size.rearrange("o (p j) -> (o p) j", j=PACK))
-        nc.gpsimd.dma_start(out=tau[:], in_=temper)
-        load_scale_rows(v_bytes, vals_scales)
-        old_sb = sb.tile([P, T], F32, name="old_sb")
-        nc.sync.dma_start(out=old_sb[:], in_=old)
+        nc.sync.dma_start(out=size_col[:], in_=size.rearrange("o (p j) -> (o p) j", j=PACK))
+        nc.gpsimd.dma_start(out=g_raw[:], in_=gout.rearrange("(p j) q -> p j q", j=PACK))
 
         def to_bf16(raw, name):
             woven = sb.tile([P, Q, PACK], BF16, name=name, align_bytes=64)
@@ -91,17 +87,15 @@ def tile_attend_btemperedpages_s_kernel(tc, query, keys_words, keys_scales, temp
                                   in_=woven[:].rearrange("p q t -> p (q t)"))
             return codes, scales
 
-        def gather(window, dtype, name):
-            picked = sb.tile([P, I], dtype, name=name, align_bytes=64)
-            nc.vector.tensor_copy(picked[:], window[:].indirect(offsets[:]))
+        def gather(window, dtype, name, tag, first=0, count=I):
+            picked = sb.tile([P, count], dtype, name=name, tag=tag, align_bytes=64)
+            nc.vector.tensor_copy(picked[:], window[:].indirect(offsets[:, first // 16:(first + count) // 16]))
             return picked
 
-        def product(rows, words, scale_bytes, name):
-            acc = ps.tile([P, I], F32, name=name)
-            nc.tensor.matmul_mx(out=acc[:], lhsT=rows[0][:].bitcast(FP8X4), lhsT_scale=rows[1][:],
-                                rhs=words[:].bitcast(FP4X4), rhs_scale=scale_bytes[:],
+        def product(acc, rows, words, scale_bytes):
+            nc.tensor.matmul_mx(out=acc, lhsT=rows[0][:].bitcast(FP8X4), lhsT_scale=rows[1][:],
+                                rhs=words.bitcast(FP4X4), rhs_scale=scale_bytes,
                                 start=True, stop=True)
-            return acc
 
         def small(name, width=G):
             return sb.tile([P, width], F32, name=name)
@@ -110,30 +104,45 @@ def tile_attend_btemperedpages_s_kernel(tc, query, keys_words, keys_scales, temp
             return sb.tile([P, I], F32, name=name)
 
         q_woven = to_bf16(q_raw, "q_woven")
+
+        size_ps = ps.tile([P, PACK, P], F32, name="size_ps", tag="first_bank")
+        for j in range(PACK):
+            nc.tensor.transpose(size_ps[:, j, :], size_col[:, j:j + 1].to_broadcast([P, P]), ident[:])
+        size_row = sb.tile([P, I], F32, name="size_row", tag="q_stage")
+        nc.scalar.activation(size_row[:].rearrange("p (n j) -> p n j", j=PACK),
+                             size_ps[:].rearrange("p j n -> p n j"), ACT.Copy, scale=512.0)
         g_woven = to_bf16(g_raw, "g_woven")
 
+        v_words = sb.tile([P, T], U16, name="v_words", tag="v_pool", align_bytes=64)
+        nc.sync.dma_start(out=v_words[:].bitcast(I32), in_=vals_words[0].bitcast(I32))
+        load_scale_rows(nc.sync, v_bytes, vals_scales)
+
+        nc.gpsimd.dma_start(out=tau[:], in_=temper)
         tau_less_one = small("tau_less_one", 1)
         tau_neg = small("tau_neg", 1)
         nc.gpsimd.tensor_scalar(tau_less_one[:], tau[:], 1.0, -1.0, ALU.mult, ALU.add)
         nc.gpsimd.tensor_scalar(tau_neg[:], tau[:], -1.0, 0.0, ALU.mult, ALU.add)
 
-        kw = gather(k_words, U16, "kw")
+        kw = gather(k_words, U16, "kw", "picked_words")
+        kb_lo = gather(k_bytes, U8, "kb_lo", "kb_lo", 0, HALF)
         q_mx = quantise(q_woven, "q")
-        kb = gather(k_bytes, U8, "kb")
-        a = product(q_mx, kw, kb, "a")
+        kb_hi = gather(k_bytes, U8, "kb_hi", "kb_hi", HALF, HALF)
+        a_lo = ps.tile([P, HALF], F32, name="a_lo", tag="first_bank")
+        a_hi = ps.tile([P, HALF], F32, name="a_hi")
+        product(a_lo[:], q_mx, kw[:, :HALF], kb_lo[:])
+        product(a_hi[:], q_mx, kw[:, HALF:], kb_hi[:])
+        a_neg = sb.tile([P, I], F32, name="a_neg", tag="a_neg", align_bytes=64)
+        least_lo = small("least_lo", 1)
+        least = small("least", 1)
+        nc.vector.tensor_scalar(a_neg[:, :HALF], a_lo[:], -1.0, None, ALU.mult, ALU.min, accum_out=least_lo[:])
+        nc.vector.tensor_scalar(a_neg[:, HALF:], a_hi[:], -1.0, least_lo[:], ALU.mult, ALU.min, accum_out=least[:])
+        x = sb.tile([P, I], F32, name="x", tag="g_stage")
+        nc.scalar.activation(x[:], a_neg[:], ACT.Exp, bias=least[:], scale=-1.0)
         g_mx = quantise(g_woven, "g")
-        a_max_neg = small("a_max_neg", 1)
-        nc.vector.tensor_reduce(a_max_neg[:], a[:], AX.X, ALU.max, negate=True)
-        x = wide("x")
-        nc.scalar.activation(x[:], a[:], ACT.Exp, bias=a_max_neg[:])
-        size_ps = ps.tile([P, PACK, P], F32, name="size_ps")
-        for j in range(PACK):
-            nc.tensor.transpose(size_ps[:, j, :], size_col[:, j:j + 1].to_broadcast([P, P]), ident[:])
-        size_row = wide("size_row")
-        nc.scalar.copy(out=size_row[:].rearrange("p (n j) -> p n j", j=PACK),
-                       in_=size_ps[:].rearrange("p j n -> p n j"))
+        vw = gather(v_words, U16, "vw", "picked_words")
+        old_sb = sb.tile([P, T], F32, name="old_sb", tag="v_pool", align_bytes=64)
+        nc.sync.dma_start(out=old_sb[:], in_=old)
 
-        vw = gather(v_words, U16, "vw")
         s = small("s")
         nc.vector.tensor_reduce(s[:], by_page(x[:]), AX.X, ALU.add)
         log_s = small("log_s")
@@ -144,37 +153,48 @@ def tile_attend_btemperedpages_s_kernel(tc, query, keys_words, keys_scales, temp
         p_over_s = small("p_over_s")
         nc.scalar.activation(p_over_s[:], log_s[:], ACT.Exp, scale=tau_less_one[:])
 
-        vb = gather(v_bytes, U8, "vb")
-        c0 = product(g_mx, vw, vb, "c0")
+        vb = sb.tile([P, I], U8, name="vb", tag="a_neg", align_bytes=64)
+        c0 = [ps.tile([P, HALF], F32, name=f"c0_{h}") for h in range(2)]
+        for h, (slots, pages) in enumerate(halves()):
+            nc.vector.tensor_copy(vb[:, slots], v_bytes[:].indirect(offsets[:, pages]))
+            product(c0[h][:], g_mx, vw[:, slots], vb[:, slots])
         s_safe = small("s_safe")
         nc.vector.tensor_scalar(s_safe[:], s[:], TINY, None, ALU.add)
         s_inv = small("s_inv")
         nc.vector.reciprocal(s_inv[:], s_safe[:])
+
         c = wide("c")
-        nc.vector.tensor_tensor(c[:], c0[:], size_row[:], ALU.mult)
         cx = wide("cx")
-        nc.vector.tensor_tensor(cx[:], c[:], x[:], ALU.mult)
         page_cx = small("page_cx")
-        nc.vector.tensor_reduce(page_cx[:], by_page(cx[:]), AX.X, ALU.add)
         mean_c = small("mean_c")
-        nc.vector.tensor_tensor(mean_c[:], page_cx[:], s_inv[:], ALU.mult)
-        u0 = wide("u0")
-        nc.vector.scalar_tensor_tensor(by_page(u0[:]), spread(mean_c[:]), tau_less_one[:], by_page(c[:]),
-                                       ALU.mult, ALU.add)
+        for h, (slots, pages) in enumerate(halves()):
+            nc.vector.tensor_tensor(c[:, slots], c0[h][:], size_row[:, slots], ALU.mult)
+        for slots, pages in halves():
+            nc.vector.tensor_tensor(cx[:, slots], c[:, slots], x[:, slots], ALU.mult)
+        for slots, pages in halves():
+            nc.vector.tensor_reduce(page_cx[:, pages], by_page(cx[:, slots]), AX.X, ALU.add)
 
         z_inv = small("z_inv", 1)
-        nc.vector.reciprocal(z_inv[:], z[:])
+        kappa = small("kappa", 1)
         weighted = small("weighted")
         total = small("total", 1)
-        nc.vector.scalar_tensor_tensor(weighted[:], mean_c[:], tau_neg[:], p[:], ALU.mult, ALU.mult,
-                                       accum_out=total[:])
-        shift = small("shift", 1)
-        nc.vector.tensor_scalar(shift[:], total[:], z_inv[:], z_inv[:], ALU.mult, ALU.mult)
+        shift = small("shift")
         u = wide("u")
-        nc.scalar.activation(u[:], u0[:], ACT.Identity, bias=shift[:], scale=z_inv[:])
         w = wide("w")
-        nc.vector.scalar_tensor_tensor(by_page(w[:]), by_page(x[:]), 512.0, spread(p_over_s[:]),
-                                       ALU.mult, ALU.mult)
+
+        def weights(slots, pages):
+            nc.vector.scalar_tensor_tensor(by_page(w[:, slots]), by_page(x[:, slots]), z_inv[:],
+                                           spread(p_over_s[:, pages]), ALU.mult, ALU.mult)
+
+        nc.vector.reciprocal(z_inv[:], z[:])
+        nc.vector.tensor_tensor(mean_c[:], page_cx[:], s_inv[:], ALU.mult)
+        nc.vector.tensor_tensor(kappa[:], z_inv[:], tau_neg[:], ALU.mult)
+        weights(*halves()[0])
+        nc.vector.scalar_tensor_tensor(weighted[:], mean_c[:], kappa[:], p[:], ALU.mult, ALU.mult,
+                                       accum_out=total[:])
+        weights(*halves()[1])
+        nc.vector.tensor_scalar(shift[:], mean_c[:], tau_less_one[:], total[:], ALU.mult, ALU.add)
+        nc.vector.tensor_tensor(by_page(u[:]), by_page(c[:]), spread(shift[:]), ALU.add)
         nc.vector.tensor_tensor(placed[:].indirect(offsets[:]), u[:], w[:], ALU.mult)
 
         col = 0

@@ -1,7 +1,6 @@
 from contextlib import ExitStack
 
 import concourse.mybir as mybir
-from concourse.masks import make_identity
 
 D, T, I, Q, G = 512, 2048, 512, 128, 32
 PAGE = I // G
@@ -23,7 +22,7 @@ AX = mybir.AxisListType
 
 TINY = 2.0 ** -64
 HALF = I // 2
-STORE_WIDTHS = (384, 640, 448, 320, 256)
+STORE_WIDTHS = (256, 320, 384, 384, 384, 320)
 
 
 def halves():
@@ -49,14 +48,17 @@ def tile_attend_btemperedpages_s_kernel(tc, query, keys_words, keys_scales, temp
         k_words = sb.tile([P, T], U16, name="k_words", tag="k_pool", align_bytes=64)
         k_bytes = sb.tile([P, T], U8, name="k_bytes", align_bytes=64)
         v_bytes = sb.tile([P, T], U8, name="v_bytes", align_bytes=64)
-        q_raw = sb.tile([P, PACK, Q], F32, name="q_raw", tag="q_stage")
+        q_raw = sb.tile([P, PACK, Q], F32, name="q_raw", tag="q_stage", align_bytes=64)
         g_raw = sb.tile([P, PACK, Q], F32, name="g_raw", tag="g_stage")
-        size_col = sb.tile([P, PACK], F32, name="size_col", tag="v_pool", align_bytes=64)
+        size_col = sb.tile([P, PACK], F32, name="size_col", tag="q_codes", align_bytes=64)
         tau = sb.tile([P, 1], F32, name="tau")
         placed = sb.tile([P, T], F32, name="placed")
         ident = sb.tile([P, P], F32, name="ident")
+        blank = sb.tile([P, P], F32, name="blank", tag="v_pool", align_bytes=64)
 
-        make_identity(nc, ident[:])
+        nc.gpsimd.memset(blank[:], 0.0)
+        nc.gpsimd.affine_select(out=ident[:], in_=blank[:], compare_op=ALU.not_equal, fill=1.0, base=0,
+                                pattern=[[-1, P]], channel_multiplier=1)
         nc.vector.memset(k_bytes[:].bitcast(I32), 0)
         nc.vector.memset(placed[:, :T // 2 - 1], 0.0)
         nc.vector.memset(placed[:, T // 2 - 1:], 0.0)
@@ -74,14 +76,14 @@ def tile_attend_btemperedpages_s_kernel(tc, query, keys_words, keys_scales, temp
         nc.sync.dma_start(out=size_col[:], in_=size.rearrange("o (p j) -> (o p) j", j=PACK))
         nc.gpsimd.dma_start(out=g_raw[:], in_=gout.rearrange("(p j) q -> p j q", j=PACK))
 
-        def to_bf16(raw, name):
-            woven = sb.tile([P, Q, PACK], BF16, name=name, align_bytes=64)
+        def to_bf16(raw, name, tag):
+            woven = sb.tile([P, Q, PACK], BF16, name=name, tag=tag, align_bytes=64)
             nc.scalar.copy(out=woven[:].rearrange("p (c i) t -> p c t i", i=4),
                            in_=raw[:].rearrange("p t (c i) -> p c t i", i=4))
             return woven
 
         def quantise(woven, name):
-            codes = sb.tile([P, Q], U32, name=name + "_codes", align_bytes=64)
+            codes = sb.tile([P, Q], U32, name=name + "_codes", tag=name + "_codes", align_bytes=64)
             scales = sb.tile([P, Q], U8, name=name + "_scales", align_bytes=64)
             nc.vector.quantize_mx(out=codes[:].bitcast(FP8X4), scales=scales[:],
                                   in_=woven[:].rearrange("p q t -> p (q t)"))
@@ -103,15 +105,15 @@ def tile_attend_btemperedpages_s_kernel(tc, query, keys_words, keys_scales, temp
         def wide(name):
             return sb.tile([P, I], F32, name=name)
 
-        q_woven = to_bf16(q_raw, "q_woven")
+        q_woven = to_bf16(q_raw, "q_woven", "q_woven")
 
-        size_ps = ps.tile([P, PACK, P], F32, name="size_ps", tag="first_bank")
+        size_ps = ps.tile([P, PACK, P], F32, name="size_ps")
         for j in range(PACK):
             nc.tensor.transpose(size_ps[:, j, :], size_col[:, j:j + 1].to_broadcast([P, P]), ident[:])
-        size_row = sb.tile([P, I], F32, name="size_row", tag="q_stage")
+        size_row = wide("size_row")
         nc.scalar.activation(size_row[:].rearrange("p (n j) -> p n j", j=PACK),
                              size_ps[:].rearrange("p j n -> p n j"), ACT.Copy, scale=512.0)
-        g_woven = to_bf16(g_raw, "g_woven")
+        g_woven = to_bf16(g_raw, "g_woven", "q_stage")
 
         v_words = sb.tile([P, T], U16, name="v_words", tag="v_pool", align_bytes=64)
         nc.sync.dma_start(out=v_words[:].bitcast(I32), in_=vals_words[0].bitcast(I32))
@@ -127,10 +129,11 @@ def tile_attend_btemperedpages_s_kernel(tc, query, keys_words, keys_scales, temp
         kb_lo = gather(k_bytes, U8, "kb_lo", "kb_lo", 0, HALF)
         q_mx = quantise(q_woven, "q")
         kb_hi = gather(k_bytes, U8, "kb_hi", "kb_hi", HALF, HALF)
-        a_lo = ps.tile([P, HALF], F32, name="a_lo", tag="first_bank")
+        a_lo = ps.tile([P, HALF], F32, name="a_lo")
         a_hi = ps.tile([P, HALF], F32, name="a_hi")
         product(a_lo[:], q_mx, kw[:, :HALF], kb_lo[:])
         product(a_hi[:], q_mx, kw[:, HALF:], kb_hi[:])
+        g_mx = quantise(g_woven, "g")
         a_neg = sb.tile([P, I], F32, name="a_neg", tag="a_neg", align_bytes=64)
         least_lo = small("least_lo", 1)
         least = small("least", 1)
@@ -138,7 +141,6 @@ def tile_attend_btemperedpages_s_kernel(tc, query, keys_words, keys_scales, temp
         nc.vector.tensor_scalar(a_neg[:, HALF:], a_hi[:], -1.0, least_lo[:], ALU.mult, ALU.min, accum_out=least[:])
         x = sb.tile([P, I], F32, name="x", tag="g_stage")
         nc.scalar.activation(x[:], a_neg[:], ACT.Exp, bias=least[:], scale=-1.0)
-        g_mx = quantise(g_woven, "g")
         vw = gather(v_words, U16, "vw", "picked_words")
         old_sb = sb.tile([P, T], F32, name="old_sb", tag="v_pool", align_bytes=64)
         nc.sync.dma_start(out=old_sb[:], in_=old)
@@ -152,16 +154,18 @@ def tile_attend_btemperedpages_s_kernel(tc, query, keys_words, keys_scales, temp
         nc.scalar.activation(p[:], log_s[:], ACT.Exp, scale=tau[:], accum_out=z[:])
         p_over_s = small("p_over_s")
         nc.scalar.activation(p_over_s[:], log_s[:], ACT.Exp, scale=tau_less_one[:])
+        s_inv = small("s_inv")
+        nc.scalar.activation(s_inv[:], log_s[:], ACT.Exp, scale=-1.0)
+        z_inv = small("z_inv", 1)
+        nc.vector.reciprocal(z_inv[:], z[:])
+        kappa = small("kappa", 1)
+        nc.scalar.activation(kappa[:], z_inv[:], ACT.Copy, scale=tau_neg[:])
 
         vb = sb.tile([P, I], U8, name="vb", tag="a_neg", align_bytes=64)
         c0 = [ps.tile([P, HALF], F32, name=f"c0_{h}") for h in range(2)]
         for h, (slots, pages) in enumerate(halves()):
             nc.vector.tensor_copy(vb[:, slots], v_bytes[:].indirect(offsets[:, pages]))
             product(c0[h][:], g_mx, vw[:, slots], vb[:, slots])
-        s_safe = small("s_safe")
-        nc.vector.tensor_scalar(s_safe[:], s[:], TINY, None, ALU.add)
-        s_inv = small("s_inv")
-        nc.vector.reciprocal(s_inv[:], s_safe[:])
 
         c = wide("c")
         cx = wide("cx")
@@ -174,11 +178,8 @@ def tile_attend_btemperedpages_s_kernel(tc, query, keys_words, keys_scales, temp
         for slots, pages in halves():
             nc.vector.tensor_reduce(page_cx[:, pages], by_page(cx[:, slots]), AX.X, ALU.add)
 
-        z_inv = small("z_inv", 1)
-        kappa = small("kappa", 1)
         weighted = small("weighted")
         total = small("total", 1)
-        shift = small("shift")
         u = wide("u")
         w = wide("w")
 
@@ -186,15 +187,12 @@ def tile_attend_btemperedpages_s_kernel(tc, query, keys_words, keys_scales, temp
             nc.vector.scalar_tensor_tensor(by_page(w[:, slots]), by_page(x[:, slots]), z_inv[:],
                                            spread(p_over_s[:, pages]), ALU.mult, ALU.mult)
 
-        nc.vector.reciprocal(z_inv[:], z[:])
-        nc.vector.tensor_tensor(mean_c[:], page_cx[:], s_inv[:], ALU.mult)
-        nc.vector.tensor_tensor(kappa[:], z_inv[:], tau_neg[:], ALU.mult)
         weights(*halves()[0])
-        nc.vector.scalar_tensor_tensor(weighted[:], mean_c[:], kappa[:], p[:], ALU.mult, ALU.mult,
+        nc.vector.scalar_tensor_tensor(weighted[:], page_cx[:], kappa[:], p_over_s[:], ALU.mult, ALU.mult,
                                        accum_out=total[:])
+        nc.vector.scalar_tensor_tensor(mean_c[:], page_cx[:], tau_less_one[:], s_inv[:], ALU.mult, ALU.mult)
         weights(*halves()[1])
-        nc.vector.tensor_scalar(shift[:], mean_c[:], tau_less_one[:], total[:], ALU.mult, ALU.add)
-        nc.vector.tensor_tensor(by_page(u[:]), by_page(c[:]), spread(shift[:]), ALU.add)
+        nc.vector.scalar_tensor_tensor(by_page(u[:]), by_page(c[:]), total[:], spread(mean_c[:]), ALU.add, ALU.add)
         nc.vector.tensor_tensor(placed[:].indirect(offsets[:]), u[:], w[:], ALU.mult)
 
         col = 0

@@ -4,6 +4,7 @@ import concourse.mybir as mybir
 
 D, T, I, Q, G = 512, 2048, 512, 128, 32
 PAGE = I // G
+HALF = I // 2
 P = 128
 PACK = 4
 FLOPS = 2 * 2 * D * I * Q
@@ -20,13 +21,10 @@ ALU = mybir.AluOpType
 ACT = mybir.ActivationFunctionType
 AX = mybir.AxisListType
 
-TINY = 2.0 ** -64
-HALF = I // 2
+LN_FLOOR = 2.0 ** -64
 STORE_WIDTHS = (256, 320, 384, 384, 384, 320)
-
-
-def halves():
-    return [(slice(h * HALF, (h + 1) * HALF), slice(h * G // 2, (h + 1) * G // 2)) for h in range(2)]
+A_NEG_BYTE = 2 * T
+HALVES = [(slice(h * HALF, (h + 1) * HALF), slice(h * G // 2, (h + 1) * G // 2)) for h in range(2)]
 
 
 def by_page(ap):
@@ -42,163 +40,175 @@ def tile_attend_btemperedpages_s_kernel(tc, query, keys_words, keys_scales, temp
     nc = tc.nc
     with ExitStack() as ctx:
         sb = ctx.enter_context(tc.tile_pool(name="sb", bufs=1))
+        shared = ctx.enter_context(tc.tile_pool(name="shared", bufs=1))
         ps = ctx.enter_context(tc.psum_pool(name="ps", bufs=1))
 
-        offsets = sb.tile([P, I // 16], U16, name="offsets")
-        k_words = sb.tile([P, T], U16, name="k_words", tag="k_pool", align_bytes=64)
-        k_bytes = sb.tile([P, T], U8, name="k_bytes", align_bytes=64)
-        v_bytes = sb.tile([P, T], U8, name="v_bytes", align_bytes=64)
-        q_raw = sb.tile([P, PACK, Q], F32, name="q_raw", tag="q_stage", align_bytes=64)
-        g_raw = sb.tile([P, PACK, Q], F32, name="g_raw", tag="g_stage")
-        size_col = sb.tile([P, PACK], F32, name="size_col", tag="q_codes", align_bytes=64)
-        tau = sb.tile([P, 1], F32, name="tau")
-        placed = sb.tile([P, T], F32, name="placed")
-        ident = sb.tile([P, P], F32, name="ident")
-        blank = sb.tile([P, P], F32, name="blank", tag="v_pool", align_bytes=64)
+        def tile(name, width, dtype=F32, tag=None):
+            return sb.tile([P, width], dtype, name=name, tag=tag or name, align_bytes=64)
 
-        nc.gpsimd.memset(blank[:], 0.0)
-        nc.gpsimd.affine_select(out=ident[:], in_=blank[:], compare_op=ALU.not_equal, fill=1.0, base=0,
+        def shared_tile(name, width, dtype, first_byte):
+            return shared.tile([P, width], dtype, name=name, align_bytes=64, offset=first_byte)
+
+        def load_scale_rows(queue, window, rows):
+            for quad in range(4):
+                queue.dma_start(out=window[32 * quad:32 * quad + 4, :].bitcast(I32),
+                                in_=rows[0, 4 * quad:4 * quad + 4, :].bitcast(I32))
+
+        def load_rows(queue, raw, rows):
+            queue.dma_start(out=raw[:].rearrange("p (t q) -> p t q", t=PACK),
+                            in_=rows.rearrange("(p t) q -> p t q", t=PACK))
+
+        def weave(woven, raw):
+            nc.scalar.copy(out=woven[:].rearrange("p (c i t) -> p c t i", i=4, t=PACK),
+                           in_=raw[:].rearrange("p (t c i) -> p c t i", i=4, t=PACK))
+
+        def quantise(codes, scales, woven):
+            nc.vector.quantize_mx(out=codes[:].bitcast(FP8X4), scales=scales[:], in_=woven[:])
+
+        def gather(picked, window, pages):
+            nc.vector.tensor_copy(picked, window[:].indirect(offsets[:, pages]))
+
+        def product(acc, codes, scales, words, scale_bytes):
+            nc.tensor.matmul_mx(out=acc[:], lhsT=codes[:].bitcast(FP8X4), lhsT_scale=scales[:],
+                                rhs=words.bitcast(FP4X4), rhs_scale=scale_bytes, start=True, stop=True)
+
+        offsets = sb.tile([P, G], U16, name="offsets")
+        k_words = tile("k_words", T, U16)
+        k_bytes = tile("k_bytes", T, U8)
+        v_bytes = tile("v_bytes", T, U8)
+        q_raw = tile("q_raw", PACK * Q, tag="q_raw_g_woven")
+        g_raw = tile("g_raw", PACK * Q, tag="g_raw_x")
+        size_cols = tile("size_cols", PACK, tag="size_cols_q_codes")
+        tau = tile("tau", 1)
+        placed = tile("placed", T)
+        ident = tile("ident", P)
+        zeros = shared_tile("zeros", P, F32, 0)
+
+        nc.gpsimd.memset(zeros[:], 0.0)
+        nc.gpsimd.affine_select(out=ident[:], in_=zeros[:], compare_op=ALU.not_equal, fill=1.0, base=0,
                                 pattern=[[-1, P]], channel_multiplier=1)
         nc.vector.memset(k_bytes[:].bitcast(I32), 0)
         nc.vector.memset(placed[:, :T // 2 - 1], 0.0)
-        nc.vector.memset(placed[:, T // 2 - 1:], 0.0)
+        nc.vector.memset(placed[:, T // 2 - 1:T - 1], 0.0)
+        nc.vector.memset(placed[:, T - 1:], 0.0)
         nc.vector.memset(v_bytes[:].bitcast(I32), 0)
 
-        def load_scale_rows(queue, tile, rows):
-            for quad in range(4):
-                queue.dma_start(out=tile[32 * quad:32 * quad + 4, :].bitcast(I32),
-                                  in_=rows[0, 4 * quad:4 * quad + 4, :].bitcast(I32))
-
-        nc.sync.dma_start(offsets[:], offs)
         nc.sync.dma_start(out=k_words[:].bitcast(I32), in_=keys_words[0].bitcast(I32))
+        nc.sync.dma_start(offsets[:], offs)
         load_scale_rows(nc.scalar, k_bytes, keys_scales)
-        nc.sync.dma_start(out=q_raw[:], in_=query.rearrange("(p j) q -> p j q", j=PACK))
-        nc.sync.dma_start(out=size_col[:], in_=size.rearrange("o (p j) -> (o p) j", j=PACK))
-        nc.gpsimd.dma_start(out=g_raw[:], in_=gout.rearrange("(p j) q -> p j q", j=PACK))
+        load_rows(nc.sync, q_raw, query)
+        nc.sync.dma_start(out=size_cols[:], in_=size.rearrange("o (p j) -> (o p) j", j=PACK))
+        load_rows(nc.gpsimd, g_raw, gout)
 
-        def to_bf16(raw, name, tag):
-            woven = sb.tile([P, Q, PACK], BF16, name=name, tag=tag, align_bytes=64)
-            nc.scalar.copy(out=woven[:].rearrange("p (c i) t -> p c t i", i=4),
-                           in_=raw[:].rearrange("p t (c i) -> p c t i", i=4))
-            return woven
-
-        def quantise(woven, name):
-            codes = sb.tile([P, Q], U32, name=name + "_codes", tag=name + "_codes", align_bytes=64)
-            scales = sb.tile([P, Q], U8, name=name + "_scales", align_bytes=64)
-            nc.vector.quantize_mx(out=codes[:].bitcast(FP8X4), scales=scales[:],
-                                  in_=woven[:].rearrange("p q t -> p (q t)"))
-            return codes, scales
-
-        def gather(window, dtype, name, tag, first=0, count=I):
-            picked = sb.tile([P, count], dtype, name=name, tag=tag, align_bytes=64)
-            nc.vector.tensor_copy(picked[:], window[:].indirect(offsets[:, first // 16:(first + count) // 16]))
-            return picked
-
-        def product(acc, rows, words, scale_bytes):
-            nc.tensor.matmul_mx(out=acc, lhsT=rows[0][:].bitcast(FP8X4), lhsT_scale=rows[1][:],
-                                rhs=words.bitcast(FP4X4), rhs_scale=scale_bytes,
-                                start=True, stop=True)
-
-        def small(name, width=G):
-            return sb.tile([P, width], F32, name=name)
-
-        def wide(name):
-            return sb.tile([P, I], F32, name=name)
-
-        q_woven = to_bf16(q_raw, "q_woven", "q_woven")
+        q_woven = tile("q_woven", PACK * Q, BF16)
+        weave(q_woven, q_raw)
 
         size_ps = ps.tile([P, PACK, P], F32, name="size_ps")
         for j in range(PACK):
-            nc.tensor.transpose(size_ps[:, j, :], size_col[:, j:j + 1].to_broadcast([P, P]), ident[:])
-        size_row = wide("size_row")
+            nc.tensor.transpose(size_ps[:, j, :], size_cols[:, j:j + 1].to_broadcast([P, P]), ident[:])
+        size_row = tile("size_row", I)
         nc.scalar.activation(size_row[:].rearrange("p (n j) -> p n j", j=PACK),
                              size_ps[:].rearrange("p j n -> p n j"), ACT.Copy, scale=512.0)
-        g_woven = to_bf16(g_raw, "g_woven", "q_stage")
+        g_woven = tile("g_woven", PACK * Q, BF16, tag="q_raw_g_woven")
+        weave(g_woven, g_raw)
 
-        v_words = sb.tile([P, T], U16, name="v_words", tag="v_pool", align_bytes=64)
+        v_words = shared_tile("v_words", T, U16, 0)
         nc.sync.dma_start(out=v_words[:].bitcast(I32), in_=vals_words[0].bitcast(I32))
         load_scale_rows(nc.sync, v_bytes, vals_scales)
 
         nc.gpsimd.dma_start(out=tau[:], in_=temper)
-        tau_less_one = small("tau_less_one", 1)
-        tau_neg = small("tau_neg", 1)
+        tau_less_one = tile("tau_less_one", 1)
+        tau_neg = tile("tau_neg", 1)
         nc.gpsimd.tensor_scalar(tau_less_one[:], tau[:], 1.0, -1.0, ALU.mult, ALU.add)
         nc.gpsimd.tensor_scalar(tau_neg[:], tau[:], -1.0, 0.0, ALU.mult, ALU.add)
 
-        kw = gather(k_words, U16, "kw", "picked_words")
-        kb_lo = gather(k_bytes, U8, "kb_lo", "kb_lo", 0, HALF)
-        q_mx = quantise(q_woven, "q")
-        kb_hi = gather(k_bytes, U8, "kb_hi", "kb_hi", HALF, HALF)
+        (lo, lo_pages), (hi, hi_pages) = HALVES
+        k_words_picked = tile("k_words_picked", I, U16)
+        k_bytes_lo = tile("k_bytes_lo", HALF, U8)
+        k_bytes_hi = tile("k_bytes_hi", HALF, U8)
+        q_codes = tile("q_codes", Q, U32, tag="size_cols_q_codes")
+        q_scales = tile("q_scales", Q, U8)
+        gather(k_words_picked[:], k_words, slice(0, G))
+        gather(k_bytes_lo[:], k_bytes, lo_pages)
+        quantise(q_codes, q_scales, q_woven)
+        gather(k_bytes_hi[:], k_bytes, hi_pages)
         a_lo = ps.tile([P, HALF], F32, name="a_lo")
         a_hi = ps.tile([P, HALF], F32, name="a_hi")
-        product(a_lo[:], q_mx, kw[:, :HALF], kb_lo[:])
-        product(a_hi[:], q_mx, kw[:, HALF:], kb_hi[:])
-        g_mx = quantise(g_woven, "g")
-        a_neg = sb.tile([P, I], F32, name="a_neg", tag="a_neg", align_bytes=64)
-        least_lo = small("least_lo", 1)
-        least = small("least", 1)
-        nc.vector.tensor_scalar(a_neg[:, :HALF], a_lo[:], -1.0, None, ALU.mult, ALU.min, accum_out=least_lo[:])
-        nc.vector.tensor_scalar(a_neg[:, HALF:], a_hi[:], -1.0, least_lo[:], ALU.mult, ALU.min, accum_out=least[:])
-        x = sb.tile([P, I], F32, name="x", tag="g_stage")
+        product(a_lo, q_codes, q_scales, k_words_picked[:, lo], k_bytes_lo[:])
+        product(a_hi, q_codes, q_scales, k_words_picked[:, hi], k_bytes_hi[:])
+        g_codes = tile("g_codes", Q, U32)
+        g_scales = tile("g_scales", Q, U8)
+        quantise(g_codes, g_scales, g_woven)
+
+        a_neg = shared_tile("a_neg", I, F32, A_NEG_BYTE)
+        least_lo = tile("least_lo", 1, tag="least_lo_v_words_picked")
+        least = tile("least", 1)
+        nc.vector.tensor_scalar(a_neg[:, lo], a_lo[:], -1.0, None, ALU.mult, ALU.min, accum_out=least_lo[:])
+        nc.vector.tensor_scalar(a_neg[:, hi], a_hi[:], -1.0, least_lo[:], ALU.mult, ALU.min, accum_out=least[:])
+        x = tile("x", I, tag="g_raw_x")
         nc.scalar.activation(x[:], a_neg[:], ACT.Exp, bias=least[:], scale=-1.0)
-        vw = gather(v_words, U16, "vw", "picked_words")
-        old_sb = sb.tile([P, T], F32, name="old_sb", tag="v_pool", align_bytes=64)
+        v_words_picked = tile("v_words_picked", I, U16, tag="least_lo_v_words_picked")
+        gather(v_words_picked[:], v_words, slice(0, G))
+
+        s = shared_tile("s", G, F32, 0)
+        nc.vector.tensor_reduce(s[:], by_page(x[:]), AX.X, ALU.add)
+        log_s = tile("log_s", G)
+        nc.scalar.activation(log_s[:], s[:], ACT.Ln, bias=LN_FLOOR)
+        p = tile("p", G)
+        z = tile("z", 1)
+        p_over_s = tile("p_over_s", G)
+        s_inv = tile("s_inv", G)
+        nc.scalar.activation(p[:], log_s[:], ACT.Exp, scale=tau[:], accum_out=z[:])
+        nc.scalar.activation(p_over_s[:], log_s[:], ACT.Exp, scale=tau_less_one[:])
+        nc.scalar.activation(s_inv[:], log_s[:], ACT.Exp, scale=-1.0)
+
+        v_bytes_picked = shared_tile("v_bytes_picked", I, U8, A_NEG_BYTE - HALF)
+        c0 = [ps.tile([P, HALF], F32, name=f"c0_{h}") for h in range(2)]
+        for h, (slots, pages) in enumerate(HALVES):
+            gather(v_bytes_picked[:, slots], v_bytes, pages)
+            product(c0[h], g_codes, g_scales, v_words_picked[:, slots], v_bytes_picked[:, slots])
+
+        old_sb = shared_tile("old_sb", T, F32, 0)
         nc.sync.dma_start(out=old_sb[:], in_=old)
 
-        s = small("s")
-        nc.vector.tensor_reduce(s[:], by_page(x[:]), AX.X, ALU.add)
-        log_s = small("log_s")
-        nc.scalar.activation(log_s[:], s[:], ACT.Ln, bias=TINY)
-        p = small("p")
-        z = small("z", 1)
-        nc.scalar.activation(p[:], log_s[:], ACT.Exp, scale=tau[:], accum_out=z[:])
-        p_over_s = small("p_over_s")
-        nc.scalar.activation(p_over_s[:], log_s[:], ACT.Exp, scale=tau_less_one[:])
-        s_inv = small("s_inv")
-        nc.scalar.activation(s_inv[:], log_s[:], ACT.Exp, scale=-1.0)
-        z_inv = small("z_inv", 1)
-        nc.vector.reciprocal(z_inv[:], z[:])
-        kappa = small("kappa", 1)
-        nc.scalar.activation(kappa[:], z_inv[:], ACT.Copy, scale=tau_neg[:])
-
-        vb = sb.tile([P, I], U8, name="vb", tag="a_neg", align_bytes=64)
-        c0 = [ps.tile([P, HALF], F32, name=f"c0_{h}") for h in range(2)]
-        for h, (slots, pages) in enumerate(halves()):
-            nc.vector.tensor_copy(vb[:, slots], v_bytes[:].indirect(offsets[:, pages]))
-            product(c0[h][:], g_mx, vw[:, slots], vb[:, slots])
-
-        c = wide("c")
-        cx = wide("cx")
-        page_cx = small("page_cx")
-        mean_c = small("mean_c")
-        for h, (slots, pages) in enumerate(halves()):
+        c = tile("c", I)
+        cx = tile("cx", I)
+        page_cx = tile("page_cx", G)
+        for h, (slots, pages) in enumerate(HALVES):
             nc.vector.tensor_tensor(c[:, slots], c0[h][:], size_row[:, slots], ALU.mult)
-        for slots, pages in halves():
+        for slots, pages in HALVES:
             nc.vector.tensor_tensor(cx[:, slots], c[:, slots], x[:, slots], ALU.mult)
-        for slots, pages in halves():
+        for slots, pages in HALVES:
             nc.vector.tensor_reduce(page_cx[:, pages], by_page(cx[:, slots]), AX.X, ALU.add)
 
-        weighted = small("weighted")
-        total = small("total", 1)
-        u = wide("u")
-        w = wide("w")
+        z_inv = tile("z_inv", 1)
+        row_parts = tile("row_parts", G)
+        row_sum = tile("row_sum", 1)
+        row_term = tile("row_term", 1)
+        page_term = tile("page_term", G)
+        left = tile("left", I)
+        right = tile("right", I)
 
-        def weights(slots, pages):
-            nc.vector.scalar_tensor_tensor(by_page(w[:, slots]), by_page(x[:, slots]), z_inv[:],
+        def left_half(slots, pages):
+            nc.vector.scalar_tensor_tensor(by_page(left[:, slots]), by_page(x[:, slots]), z_inv[:],
                                            spread(p_over_s[:, pages]), ALU.mult, ALU.mult)
 
-        weights(*halves()[0])
-        nc.vector.scalar_tensor_tensor(weighted[:], page_cx[:], kappa[:], p_over_s[:], ALU.mult, ALU.mult,
-                                       accum_out=total[:])
-        nc.vector.scalar_tensor_tensor(mean_c[:], page_cx[:], tau_less_one[:], s_inv[:], ALU.mult, ALU.mult)
-        weights(*halves()[1])
-        nc.vector.scalar_tensor_tensor(by_page(u[:]), by_page(c[:]), total[:], spread(mean_c[:]), ALU.add, ALU.add)
-        nc.vector.tensor_tensor(placed[:].indirect(offsets[:]), u[:], w[:], ALU.mult)
+        nc.vector.reciprocal(z_inv[:], z[:])
+        nc.vector.scalar_tensor_tensor(row_parts[:], page_cx[:], tau_neg[:], p_over_s[:], ALU.mult, ALU.mult,
+                                       accum_out=row_sum[:])
+        nc.vector.scalar_tensor_tensor(page_term[:], page_cx[:], tau_less_one[:], s_inv[:], ALU.mult, ALU.mult)
+        left_half(lo, lo_pages)
+        nc.vector.tensor_tensor(row_term[:], row_sum[:], z_inv[:], ALU.mult)
+        left_half(hi, hi_pages)
+        nc.vector.scalar_tensor_tensor(by_page(right[:]), by_page(c[:]), row_term[:], spread(page_term[:]),
+                                       ALU.add, ALU.add)
+        nc.vector.tensor_tensor(placed[:].indirect(offsets[:]), right[:], left[:], ALU.mult)
 
-        col = 0
+        first = 0
         for n, width in enumerate(STORE_WIDTHS):
-            result = sb.tile([P, width], F32, name=f"result{n}")
-            nc.vector.tensor_tensor(result[:], old_sb[:, col:col + width], placed[:, col:col + width], ALU.add)
+            cols = slice(first, first + width)
+            result = tile(f"result{n}", width)
+            nc.vector.tensor_tensor(result[:], old_sb[:, cols], placed[:, cols], ALU.add)
             queue = nc.sync if n % 2 == 0 else nc.scalar
-            queue.dma_start(out=out[:, col:col + width], in_=result[:])
-            col = col + width
+            queue.dma_start(out=out[:, cols], in_=result[:])
+            first = first + width

from contextlib import ExitStack

import concourse.mybir as mybir

D, T, I, Q, G = 512, 2048, 512, 128, 32
PAGE = I // G
HALF = I // 2
P = 128
PACK = 4
FLOPS = 2 * 2 * D * I * Q

F32 = mybir.dt.float32
BF16 = mybir.dt.bfloat16
I32 = mybir.dt.int32
U32 = mybir.dt.uint32
U16 = mybir.dt.uint16
U8 = mybir.dt.uint8
FP8X4 = mybir.dt.float8_e4m3fn_x4
FP4X4 = mybir.dt.float4_e2m1fn_x4
ALU = mybir.AluOpType
ACT = mybir.ActivationFunctionType
AX = mybir.AxisListType

LN_FLOOR = 2.0 ** -64
STORE_WIDTHS = (256, 320, 384, 384, 384, 320)
A_NEG_BYTE = 2 * T
HALVES = [(slice(h * HALF, (h + 1) * HALF), slice(h * G // 2, (h + 1) * G // 2)) for h in range(2)]


def by_page(ap):
    return ap.rearrange("p (g j) -> p g j", j=PAGE)


def spread(ap):
    return ap.unsqueeze(2).to_broadcast([P, ap.shape[1], PAGE])


def tile_attend_btemperedpages_s_kernel(tc, query, keys_words, keys_scales, temper, gout,
                                         vals_words, vals_scales, size, old, offs, out):
    nc = tc.nc
    with ExitStack() as ctx:
        sb = ctx.enter_context(tc.tile_pool(name="sb", bufs=1))
        shared = ctx.enter_context(tc.tile_pool(name="shared", bufs=1))
        ps = ctx.enter_context(tc.psum_pool(name="ps", bufs=1))

        def tile(name, width, dtype=F32, tag=None):
            return sb.tile([P, width], dtype, name=name, tag=tag or name, align_bytes=64)

        def shared_tile(name, width, dtype, first_byte):
            return shared.tile([P, width], dtype, name=name, align_bytes=64, offset=first_byte)

        def load_scale_rows(queue, window, rows):
            for quad in range(4):
                queue.dma_start(out=window[32 * quad:32 * quad + 4, :].bitcast(I32),
                                in_=rows[0, 4 * quad:4 * quad + 4, :].bitcast(I32))

        def load_rows(queue, raw, rows):
            queue.dma_start(out=raw[:].rearrange("p (t q) -> p t q", t=PACK),
                            in_=rows.rearrange("(p t) q -> p t q", t=PACK))

        def weave(woven, raw):
            nc.scalar.copy(out=woven[:].rearrange("p (c i t) -> p c t i", i=4, t=PACK),
                           in_=raw[:].rearrange("p (t c i) -> p c t i", i=4, t=PACK))

        def quantise(codes, scales, woven):
            nc.vector.quantize_mx(out=codes[:].bitcast(FP8X4), scales=scales[:], in_=woven[:])

        def gather(picked, window, pages):
            nc.vector.tensor_copy(picked, window[:].indirect(offsets[:, pages]))

        def product(acc, codes, scales, words, scale_bytes):
            nc.tensor.matmul_mx(out=acc[:], lhsT=codes[:].bitcast(FP8X4), lhsT_scale=scales[:],
                                rhs=words.bitcast(FP4X4), rhs_scale=scale_bytes, start=True, stop=True)

        offsets = sb.tile([P, G], U16, name="offsets")
        k_words = tile("k_words", T, U16)
        k_bytes = tile("k_bytes", T, U8)
        v_bytes = tile("v_bytes", T, U8)
        q_raw = tile("q_raw", PACK * Q, tag="q_raw_g_woven")
        g_raw = tile("g_raw", PACK * Q, tag="g_raw_x")
        size_cols = tile("size_cols", PACK, tag="size_cols_q_codes")
        tau = tile("tau", 1)
        placed = tile("placed", T)
        ident = tile("ident", P)
        zeros = shared_tile("zeros", P, F32, 0)

        nc.gpsimd.memset(zeros[:], 0.0)
        nc.gpsimd.affine_select(out=ident[:], in_=zeros[:], compare_op=ALU.not_equal, fill=1.0, base=0,
                                pattern=[[-1, P]], channel_multiplier=1)
        nc.vector.memset(k_bytes[:].bitcast(I32), 0)
        nc.vector.memset(placed[:, :T // 2 - 1], 0.0)
        nc.vector.memset(placed[:, T // 2 - 1:T - 1], 0.0)
        nc.vector.memset(placed[:, T - 1:], 0.0)
        nc.vector.memset(v_bytes[:].bitcast(I32), 0)

        nc.sync.dma_start(out=k_words[:].bitcast(I32), in_=keys_words[0].bitcast(I32))
        nc.sync.dma_start(offsets[:], offs)
        load_scale_rows(nc.scalar, k_bytes, keys_scales)
        load_rows(nc.sync, q_raw, query)
        nc.sync.dma_start(out=size_cols[:], in_=size.rearrange("o (p j) -> (o p) j", j=PACK))
        load_rows(nc.gpsimd, g_raw, gout)

        q_woven = tile("q_woven", PACK * Q, BF16)
        weave(q_woven, q_raw)

        size_ps = ps.tile([P, PACK, P], F32, name="size_ps")
        for j in range(PACK):
            nc.tensor.transpose(size_ps[:, j, :], size_cols[:, j:j + 1].to_broadcast([P, P]), ident[:])
        size_row = tile("size_row", I)
        nc.scalar.activation(size_row[:].rearrange("p (n j) -> p n j", j=PACK),
                             size_ps[:].rearrange("p j n -> p n j"), ACT.Copy, scale=512.0)
        g_woven = tile("g_woven", PACK * Q, BF16, tag="q_raw_g_woven")
        weave(g_woven, g_raw)

        v_words = shared_tile("v_words", T, U16, 0)
        nc.sync.dma_start(out=v_words[:].bitcast(I32), in_=vals_words[0].bitcast(I32))
        load_scale_rows(nc.sync, v_bytes, vals_scales)

        nc.gpsimd.dma_start(out=tau[:], in_=temper)
        tau_less_one = tile("tau_less_one", 1)
        tau_neg = tile("tau_neg", 1)
        nc.gpsimd.tensor_scalar(tau_less_one[:], tau[:], 1.0, -1.0, ALU.mult, ALU.add)
        nc.gpsimd.tensor_scalar(tau_neg[:], tau[:], -1.0, 0.0, ALU.mult, ALU.add)

        (lo, lo_pages), (hi, hi_pages) = HALVES
        k_words_picked = tile("k_words_picked", I, U16)
        k_bytes_lo = tile("k_bytes_lo", HALF, U8)
        k_bytes_hi = tile("k_bytes_hi", HALF, U8)
        q_codes = tile("q_codes", Q, U32, tag="size_cols_q_codes")
        q_scales = tile("q_scales", Q, U8)
        gather(k_words_picked[:], k_words, slice(0, G))
        gather(k_bytes_lo[:], k_bytes, lo_pages)
        quantise(q_codes, q_scales, q_woven)
        gather(k_bytes_hi[:], k_bytes, hi_pages)
        a_lo = ps.tile([P, HALF], F32, name="a_lo")
        a_hi = ps.tile([P, HALF], F32, name="a_hi")
        product(a_lo, q_codes, q_scales, k_words_picked[:, lo], k_bytes_lo[:])
        product(a_hi, q_codes, q_scales, k_words_picked[:, hi], k_bytes_hi[:])
        g_codes = tile("g_codes", Q, U32)
        g_scales = tile("g_scales", Q, U8)
        quantise(g_codes, g_scales, g_woven)

        a_neg = shared_tile("a_neg", I, F32, A_NEG_BYTE)
        least_lo = tile("least_lo", 1, tag="least_lo_v_words_picked")
        least = tile("least", 1)
        nc.vector.tensor_scalar(a_neg[:, lo], a_lo[:], -1.0, None, ALU.mult, ALU.min, accum_out=least_lo[:])
        nc.vector.tensor_scalar(a_neg[:, hi], a_hi[:], -1.0, least_lo[:], ALU.mult, ALU.min, accum_out=least[:])
        x = tile("x", I, tag="g_raw_x")
        nc.scalar.activation(x[:], a_neg[:], ACT.Exp, bias=least[:], scale=-1.0)
        v_words_picked = tile("v_words_picked", I, U16, tag="least_lo_v_words_picked")
        gather(v_words_picked[:], v_words, slice(0, G))

        s = shared_tile("s", G, F32, 0)
        nc.vector.tensor_reduce(s[:], by_page(x[:]), AX.X, ALU.add)
        log_s = tile("log_s", G)
        nc.scalar.activation(log_s[:], s[:], ACT.Ln, bias=LN_FLOOR)
        p = tile("p", G)
        z = tile("z", 1)
        p_over_s = tile("p_over_s", G)
        s_inv = tile("s_inv", G)
        nc.scalar.activation(p[:], log_s[:], ACT.Exp, scale=tau[:], accum_out=z[:])
        nc.scalar.activation(p_over_s[:], log_s[:], ACT.Exp, scale=tau_less_one[:])
        nc.scalar.activation(s_inv[:], log_s[:], ACT.Exp, scale=-1.0)

        v_bytes_picked = shared_tile("v_bytes_picked", I, U8, A_NEG_BYTE - HALF)
        c0 = [ps.tile([P, HALF], F32, name=f"c0_{h}") for h in range(2)]
        for h, (slots, pages) in enumerate(HALVES):
            gather(v_bytes_picked[:, slots], v_bytes, pages)
            product(c0[h], g_codes, g_scales, v_words_picked[:, slots], v_bytes_picked[:, slots])

        old_sb = shared_tile("old_sb", T, F32, 0)
        nc.sync.dma_start(out=old_sb[:], in_=old)

        c = tile("c", I)
        cx = tile("cx", I)
        page_cx = tile("page_cx", G)
        for h, (slots, pages) in enumerate(HALVES):
            nc.vector.tensor_tensor(c[:, slots], c0[h][:], size_row[:, slots], ALU.mult)
        for slots, pages in HALVES:
            nc.vector.tensor_tensor(cx[:, slots], c[:, slots], x[:, slots], ALU.mult)
        for slots, pages in HALVES:
            nc.vector.tensor_reduce(page_cx[:, pages], by_page(cx[:, slots]), AX.X, ALU.add)

        z_inv = tile("z_inv", 1)
        row_parts = tile("row_parts", G)
        row_sum = tile("row_sum", 1)
        row_term = tile("row_term", 1)
        page_term = tile("page_term", G)
        left = tile("left", I)
        right = tile("right", I)

        def left_half(slots, pages):
            nc.vector.scalar_tensor_tensor(by_page(left[:, slots]), by_page(x[:, slots]), z_inv[:],
                                           spread(p_over_s[:, pages]), ALU.mult, ALU.mult)

        nc.vector.reciprocal(z_inv[:], z[:])
        nc.vector.scalar_tensor_tensor(row_parts[:], page_cx[:], tau_neg[:], p_over_s[:], ALU.mult, ALU.mult,
                                       accum_out=row_sum[:])
        nc.vector.scalar_tensor_tensor(page_term[:], page_cx[:], tau_less_one[:], s_inv[:], ALU.mult, ALU.mult)
        left_half(lo, lo_pages)
        nc.vector.tensor_tensor(row_term[:], row_sum[:], z_inv[:], ALU.mult)
        left_half(hi, hi_pages)
        nc.vector.scalar_tensor_tensor(by_page(right[:]), by_page(c[:]), row_term[:], spread(page_term[:]),
                                       ALU.add, ALU.add)
        nc.vector.tensor_tensor(placed[:].indirect(offsets[:]), right[:], left[:], ALU.mult)

        first = 0
        for n, width in enumerate(STORE_WIDTHS):
            cols = slice(first, first + width)
            result = tile(f"result{n}", width)
            nc.vector.tensor_tensor(result[:], old_sb[:, cols], placed[:, cols], ALU.add)
            queue = nc.sync if n % 2 == 0 else nc.scalar
            queue.dma_start(out=out[:, cols], in_=result[:])
            first = first + width
